import numpy as np
import ml_dtypes


def mxq(x, axis, fmt="e4m3"):
    dtype, down = {"e4m3": (ml_dtypes.float8_e4m3fn, 7), "e5m2": (ml_dtypes.float8_e5m2, 14)}[fmt]
    v = np.moveaxis(np.asarray(x, np.float32).astype(ml_dtypes.bfloat16).astype(np.float64), axis, -1)
    blocks = v.reshape(v.shape[:-1] + (-1, 32))
    amax = np.abs(blocks).max(-1, keepdims=True)
    byte = np.maximum(np.where(amax > 0, np.frexp(amax)[1] - 1 + 127, 0) - down, 1)
    scale = np.exp2(byte - 127.0)
    codes = (blocks / scale).astype(np.float32).astype(dtype).astype(np.float64)
    return np.moveaxis((codes * scale).reshape(v.shape), -1, axis)


WIDE = False


def mx_kscale(k):
    if not WIDE:
        return np.ones(k)
    levels = np.array([10, -10, 5, -5, 0])
    if k % 512:
        return np.exp2(np.random.permutation(np.resize(levels, k // 32))).repeat(32)
    a = np.empty((k // 512, 16))
    for p in range(k // 512):
        a[p, :8] = np.random.permutation(np.resize(levels, 8))
        for g in range(8):
            far = levels[np.abs(levels - a[p, g]) >= 10]
            a[p, g + 8] = far[np.random.randint(len(far))]
    return np.exp2(a.ravel()).repeat(32)


def f64(x):
    return np.asarray(x).astype(np.float64)


def striped(idx):
    return np.tile(idx.reshape(-1, 16).T, (8, 1)).astype(np.uint16)


def unstriped(offs):
    return offs[:16].T.reshape(-1).astype(np.int64)


E2M1 = np.array([0.0, 0.5, 1.0, 1.5, 2.0, 3.0, 4.0, 6.0, -0.0, -0.5, -1.0, -1.5, -2.0, -3.0, -4.0, -6.0])


def pack_weight(w, fmt):
    k, n = w.shape
    w = f64(np.asarray(w, np.float32).astype(ml_dtypes.bfloat16)).reshape(k // 32, 32, n)
    amax = np.abs(w).max(1)
    if fmt == "e4m3":
        byte = np.frexp(amax)[1] - 1 + 127 - 7
    else:
        mant, ex = np.frexp(amax / 6.0)
        byte = np.where(mant > 0.5, ex, ex - 1) + 127
    byte = np.clip(np.where(amax > 0, byte, 1), 1, 254)
    scaled = (w * np.exp2(127.0 - byte)[:, None, :]).reshape(k, n).astype(np.float32)
    by_word = np.ascontiguousarray(scaled.reshape(k // 512, 128, 4, n).transpose(0, 1, 3, 2))
    if fmt == "e4m3":
        words = by_word.astype(ml_dtypes.float8_e4m3fn).view(np.uint8)
    else:
        c = by_word.astype(ml_dtypes.float4_e2m1fn).view(np.uint8) & 0xF
        words = (c[..., 0::2] | (c[..., 1::2] << 4)).reshape(k // 512, 128, 2 * n)
    return np.ascontiguousarray(words), np.ascontiguousarray(byte.astype(np.uint8).reshape(k // 512, 16, n))


def unpack_weight(words, scales, fmt):
    g, _, n = scales.shape
    words = np.ascontiguousarray(words).reshape(g, 128, n, -1)
    if fmt == "e4m3":
        vals = words.view(ml_dtypes.float8_e4m3fn).astype(np.float64)
    else:
        nib = np.empty((g, 128, n, 4), np.uint8)
        nib[..., 0::2] = words & 0xF
        nib[..., 1::2] = words >> 4
        vals = E2M1[nib]
    vals = vals * np.repeat(np.exp2(scales.astype(np.float64) - 127.0), 8, axis=1)[..., None]
    return vals.transpose(0, 1, 3, 2).reshape(g * 512, n)


def gelu(v):
    return 0.5 * v * (1.0 + np.tanh(np.sqrt(2.0 / np.pi) * (v + 0.044715 * v**3)))


def striped8(idx):
    return np.concatenate([v.reshape(-1, 16).T for v in idx]).astype(np.uint16)


def unstriped8(offs):
    return np.stack([offs[16 * g:16 * g + 16].T.reshape(-1) for g in range(8)]).astype(np.int64)


def runs(v, idx8):
    k = np.arange(v.shape[0])
    return v[k[:, None], idx8[k % 512 // 64]]


K, H, N, T, S, P, BANDS = 1536, 1024, 512, 2048, 1024, 512, 8

def setup_inputs():
    n = lambda shape: np.random.standard_normal(shape)
    s = mx_kscale(K)[:, None]
    u = mx_kscale(H)[:, None]
    d = {}
    d["tab_words"], d["tab_scales"] = pack_weight(n((K, T)) * s, "e4m3")
    d["offs"] = striped8(np.stack([np.random.permutation(T)[:S] for _ in range(BANDS)]))
    d["pos1"] = striped(np.random.permutation(S)[:P])
    d["pos2"] = striped(np.random.permutation(S)[:P])
    d["w1"] = (1.8 * n((K, H)) / K ** 0.5 / s).astype(np.float32)
    d["gain"] = (u[:, 0] * np.exp(0.3 * n(H))).astype(np.float32)
    d["w2_words"], d["w2_scales"] = pack_weight(n((H, N)) / H ** 0.5 / u, "e2m1")
    d["w3"] = (1.5 * n((H, N)) / H ** 0.5 / u).astype(np.float32)
    return d

def reference(tab_words, tab_scales, offs, pos1, pos2, w1, gain, w2_words, w2_scales, w3):
    v = runs(unpack_weight(tab_words, tab_scales, "e4m3"), unstriped8(offs))
    a = mxq(f64(w1), 0, "e4m3").T @ v
    h = f64(gain)[:, None] * (a / (1.0 + np.exp(-a)))
    climb = h[:, unstriped(pos1)]
    descent = h[:, unstriped(pos2)]
    both = mxq(climb + descent, 0, "e4m3")
    apart = mxq(np.abs(climb - descent), 0, "e4m3")
    w2 = unpack_weight(w2_words, w2_scales, "e2m1")
    worth = w2.T @ both
    contrast = mxq(f64(w3), 0, "e4m3").T @ apart
    return worth * (1.0 / (1.0 + np.exp(-contrast)))

@@ -1,0 +1,285 @@
+from contextlib import ExitStack
+
+import concourse.mybir as mybir
+
+K, H, N, T, S, M = 1536, 1024, 512, 2048, 1024, 512
+FLOPS = 2 * K * H * S + 2 * 2 * H * N * M
+
+F32 = mybir.dt.float32
+BF16 = mybir.dt.bfloat16
+I32 = mybir.dt.int32
+U32 = mybir.dt.uint32
+U16 = mybir.dt.uint16
+U8 = mybir.dt.uint8
+FP8X4 = mybir.dt.float8_e4m3fn_x4
+FP4X4 = mybir.dt.float4_e2m1fn_x4
+ALU = mybir.AluOpType
+ACT = mybir.ActivationFunctionType
+
+P = 128
+PACK = 4
+KP = P * PACK
+BANK = 512
+K_PASSES = K // KP
+H_PASSES = H // KP
+SCALE_ROW = (0, 8, 4)
+HALF = M // 2
+
+
+def tile_list_balloon_leg_values_kernel(
+    tc, tab_words, tab_scales, offs, pos1, pos2, w1, gain, w2_words, w2_scales, w3, out
+):
+    nc = tc.nc
+    with ExitStack() as ctx:
+        lists = ctx.enter_context(tc.tile_pool(name="lists", bufs=1))
+        keep = ctx.enter_context(tc.tile_pool(name="keep", bufs=1))
+        raws = ctx.enter_context(tc.tile_pool(name="raws", bufs=2))
+        rounded = ctx.enter_context(tc.tile_pool(name="rounded", bufs=1))
+        rows = ctx.enter_context(tc.tile_pool(name="rows", bufs=8))
+        tables = ctx.enter_context(tc.tile_pool(name="tables", bufs=2))
+        picks = ctx.enter_context(tc.tile_pool(name="picks", bufs=1))
+        psum = ctx.enter_context(tc.psum_pool(name="psum", bufs=8))
+
+        offs_sb = lists.tile([P, S // 16], U16, name="offs_sb")
+        pos1_sb = lists.tile([P, M // 16], U16, name="pos1_sb")
+        pos2_sb = lists.tile([P, M // 16], U16, name="pos2_sb")
+        nc.sync.dma_start(offs_sb[:], offs)
+
+        gain_sb = keep.tile([P, H_PASSES, PACK], F32, name="gain_sb")
+        nc.scalar.dma_start(gain_sb[:], gain.rearrange("(b p t) -> p b t", p=P, t=PACK))
+
+        tab_bytes = keep.tile([P, T], U8, name="tab_bytes")
+        nc.vector.memset(tab_bytes[:].bitcast(I32), 0)
+
+        def load_rows(pool, weight, a, cols, name):
+            raw = pool.tile([P, PACK, BANK], F32, name=name, tag="slot", align_bytes=64)
+            nc.sync.dma_start(raw[:], weight[KP * a : KP * (a + 1), cols].rearrange("(p j) c -> p j c", j=PACK))
+            return raw
+
+        def load_table(a):
+            words = tables.tile([P, T], U32, name="tab%d" % a, tag="slot", align_bytes=64)
+            nc.sync.dma_start(words[:].bitcast(I32), tab_words[a].rearrange("p t i -> p (t i)").bitcast(I32))
+            return words
+
+        tab_sb = [load_table(0)]
+        nc.sync.dma_start(pos1_sb[:], pos1)
+        nc.sync.dma_start(pos2_sb[:], pos2)
+        by_parity = tab_scales.bitcast(I32).rearrange("a (g s) t -> s g a t", s=2)
+        for s in range(2):
+            nc.sync.dma_start(tab_bytes[s:P:8, :].bitcast(I32), by_parity[s, :, 0:2, :])
+            nc.sync.dma_start(tab_bytes[4 + s : P : 16, :].bitcast(I32), by_parity[s, :, 2, :])
+        w1_raw = {(0, 0): load_rows(raws, w1, 0, slice(0, KP), "w1_raw00")}
+        for a in range(1, K_PASSES):
+            tab_sb.append(load_table(a))
+            w1_raw[a, 0] = load_rows(raws, w1, a, slice(0, KP), "w1_raw%d0" % a)
+        w3_raw = [load_rows(tables, w3, b, slice(0, N), "w3_raw%d" % b) for b in range(H_PASSES)]
+        for a in range(K_PASSES):
+            w1_raw[a, 1] = load_rows(raws, w1, a, slice(KP, 2 * KP), "w1_raw%d1" % a)
+        w2_codes = raws.tile([P, H_PASSES, 2 * N], U8, name="w2_codes", tag="slot", align_bytes=64)
+        nc.sync.dma_start(w2_codes[:].bitcast(I32), w2_words.bitcast(I32).rearrange("b p c -> p b c"))
+        w2_plane = raws.tile([P, H_PASSES, N], U8, name="w2_plane", tag="slot", align_bytes=64)
+        nc.gpsimd.memset(w2_plane[:].bitcast(I32), 0)
+        for d in range(4):
+            nc.sync.dma_start(
+                w2_plane[32 * d : 32 * d + 4, :, :].bitcast(I32),
+                w2_scales.bitcast(I32)[:, 4 * d : 4 * d + 4, :].rearrange("b q c -> q b c"),
+            )
+
+        half_gain = keep.tile([P, H_PASSES * PACK], F32, name="half_gain")
+        nc.vector.tensor_scalar_mul(half_gain[:], gain_sb[:].rearrange("p b t -> p (b t)"), 0.5)
+        gain_rows = []
+
+        def spread_gain(b, width):
+            for r in range(PACK * b, PACK * (b + 1)):
+                g = keep.tile([P, width], F32, name="gain_row%d" % r)
+                nc.scalar.copy(g[:], half_gain[:, r : r + 1].to_broadcast([P, width]))
+                gain_rows.append(g)
+
+        spread_gain(0, M)
+
+        picked_bytes = keep.tile([P, S], U8, name="picked_bytes")
+        nc.vector.tensor_copy(picked_bytes[:], tab_bytes[:].indirect(offs_sb[:]))
+        v_plane = keep.tile([P, S], U8, name="v_plane", align_bytes=64)
+        nc.vector.tensor_copy(v_plane[:].bitcast(I32), picked_bytes[:].bitcast(I32))
+        for s in range(2):
+            nc.sync.dma_start(
+                v_plane[2 + s : 110 : 4, :].bitcast(I32), picked_bytes[16 + s : 124 : 4, :].bitcast(I32)
+            )
+
+        def quantize(source, name):
+            width = source.shape[1] // PACK
+            codes = keep.tile([P, width], U32, name=name + "_codes", align_bytes=64)
+            plane = keep.tile([P, width], U8, name=name + "_plane", align_bytes=64)
+            nc.vector.quantize_mx(out=codes[:].bitcast(FP8X4), scales=plane[:], in_=source)
+            return codes, plane
+
+        def rounded_tile(width, name, slot):
+            return rounded.tile([P, PACK * width], BF16, name=name, tag="bf%d" % slot, align_bytes=64)
+
+        def round_w1(a, b, copy):
+            dealt = rounded_tile(BANK, "w1_bf%d%d" % (a, b), (K_PASSES * b + a) % 2)
+            copy(
+                dealt[:].rearrange("p (t m j) -> p m j t", t=PACK, j=PACK),
+                w1_raw[a, b][:].rearrange("p j (m t) -> p m j t", t=PACK),
+            )
+            return quantize(dealt[:], "w1_%d%d" % (a, b))
+
+        def round_w3(b, copy, slot):
+            w3_bf = rounded_tile(N, "w3_bf%d" % b, slot)
+            copy(woven(w3_bf[:]), apart_rows(w3_raw[b][:]))
+            return quantize(w3_bf[:], "w3_%d" % b)
+
+        def woven(tile):
+            return tile.rearrange("p (c i t) -> p c t i", i=4, t=PACK)
+
+        def apart_rows(tile):
+            return tile.rearrange("p t (c i) -> p c t i", i=4)
+
+        def first_stage_pass(banks, a, w1_q):
+            codes, plane = w1_q
+            for t in range(PACK):
+                cols = slice(P * t, P * (t + 1))
+                for half in range(S // BANK):
+                    j = slice(BANK * half, BANK * (half + 1))
+                    nc.tensor.matmul_mx(
+                        out=banks[t][half][:],
+                        lhsT=codes[:, cols].bitcast(FP8X4),
+                        lhsT_scale=plane[:, cols],
+                        rhs=v_codes[a][:, j].bitcast(FP8X4),
+                        rhs_scale=v_plane[SCALE_ROW[a] : P, j],
+                        start=(a == 0),
+                        stop=(a == K_PASSES - 1),
+                    )
+
+        def new_banks(b):
+            return [
+                [psum.tile([P, BANK], F32, name="acc%d%d%d" % (b, t, half), tag="bank") for half in range(S // BANK)]
+                for t in range(PACK)
+            ]
+
+        def silu_rows(banks, b, t):
+            h = rows.tile([P, S], F32, name="h%d%d" % (b, t), tag="h")
+            for half in range(S // BANK):
+                nc.scalar.activation(h[:, BANK * half : BANK * (half + 1)], banks[t][half][:], ACT.Silu)
+            return h
+
+        def new_picks(name, width):
+            return [
+                picks.tile([P, PACK, width], F32, name="climb" + name, tag="climb"),
+                picks.tile([P, PACK, width], F32, name="descent" + name, tag="descent"),
+                picks.tile([P, PACK, width], F32, name="diff" + name),
+            ]
+
+        def pick(h, b, t, m0, tiles):
+            climb, descent, diff = tiles
+            width = climb.shape[2]
+            g = gain_rows[PACK * b + t][:, 0:width]
+            for dst, pos in ((climb, pos1_sb), (descent, pos2_sb)):
+                nc.vector.tensor_tensor(
+                    dst[:, t, :], h[:].indirect(pos[:, m0 // 16 : (m0 + width) // 16]), g, ALU.mult
+                )
+            nc.vector.tensor_tensor(diff[:, t, :], climb[:, t, :], descent[:, t, :], ALU.subtract)
+
+        def make_both(tiles, name, slot):
+            climb, descent = tiles[0:2]
+            both = rounded_tile(climb.shape[2], "both" + name, slot)
+            nc.vector.tensor_tensor(woven(both[:]), apart_rows(climb[:]), apart_rows(descent[:]), ALU.add)
+            return quantize(both[:], "both" + name)
+
+        def make_apart(tiles, name, slot):
+            diff = tiles[2]
+            width = diff.shape[2]
+            apart = rounded_tile(width, "apart" + name, slot)
+            for m0 in range(0, width, HALF):
+                nc.scalar.activation(
+                    woven(apart[:, PACK * m0 : PACK * (m0 + HALF)]), apart_rows(diff[:, :, m0 : m0 + HALF]), ACT.Abs
+                )
+            return quantize(apart[:], "apart" + name)
+
+        v_codes = []
+        first_banks = new_banks(0)
+        for a in range(K_PASSES):
+            picked = keep.tile([P, S], U32, name="v%d" % a, align_bytes=64)
+            nc.vector.tensor_copy(picked[:], tab_sb[a][:].indirect(offs_sb[:]))
+            v_codes.append(picked)
+            copy = nc.vector.tensor_copy if a == K_PASSES - 1 else nc.scalar.copy
+            first_stage_pass(first_banks, a, round_w1(a, 0, copy))
+        w3_q = [round_w3(0, nc.vector.tensor_copy, 2)]
+        spread_gain(1, HALF)
+
+        first_picks = new_picks("0", M)
+        w1_q = []
+        for t in range(PACK):
+            pick(silu_rows(first_banks, 0, t), 0, t, 0, first_picks)
+            if t > 0:
+                w1_q.append(round_w1(t - 1, 1, nc.scalar.copy))
+        second_banks = new_banks(1)
+        for a in range(K_PASSES):
+            first_stage_pass(second_banks, a, w1_q[a])
+        both0 = make_both(first_picks, "0", 1)
+        h_second = [silu_rows(second_banks, 1, t) for t in range(PACK)]
+        apart0 = make_apart(first_picks, "0", 0)
+        w3_q.append(round_w3(1, nc.scalar.copy, 1))
+
+        def second_stage_pass(worth, contrast, b, both_q, apart_q, m0):
+            for pair in range(2):
+                for u in range(2):
+                    nt = 2 * pair + u
+                    n_cols = slice(P * nt, P * (nt + 1))
+                    for c in range(HALF // P):
+                        m_cols = slice(m0 + P * c, m0 + P * (c + 1))
+                        nc.tensor.matmul_mx(
+                            out=worth[pair][:, u, P * c : P * (c + 1)],
+                            lhsT=w2_codes[:, b, 2 * P * nt : 2 * P * (nt + 1)].bitcast(FP4X4),
+                            lhsT_scale=w2_plane[:, b, n_cols],
+                            rhs=both_q[0][:, m_cols].bitcast(FP8X4),
+                            rhs_scale=both_q[1][:, m_cols],
+                            start=(b == 0 and u == 0 and c == 0),
+                            stop=(b == H_PASSES - 1 and u == 1 and c == HALF // P - 1),
+                        )
+            for pair in range(2):
+                for u in range(2):
+                    nt = 2 * pair + u
+                    n_cols = slice(P * nt, P * (nt + 1))
+                    m_cols = slice(m0, m0 + HALF)
+                    nc.tensor.matmul_mx(
+                        out=contrast[pair][:, u, :],
+                        lhsT=w3_q[b][0][:, n_cols].bitcast(FP8X4),
+                        lhsT_scale=w3_q[b][1][:, n_cols],
+                        rhs=apart_q[0][:, m_cols].bitcast(FP8X4),
+                        rhs_scale=apart_q[1][:, m_cols],
+                        start=(b == 0 and u == 0),
+                        stop=(b == H_PASSES - 1 and u == 1),
+                    )
+
+        sums = []
+        for half in range(2):
+            worth = [psum.tile([P, 2, HALF], F32, name="worth%d%d" % (half, pair), tag="bank") for pair in range(2)]
+            contrast = [
+                psum.tile([P, 2, HALF], F32, name="contrast%d%d" % (half, pair), tag="bank") for pair in range(2)
+            ]
+            second_stage_pass(worth, contrast, 0, both0, apart0, HALF * half)
+            sums.append((worth, contrast))
+
+        for half in range(2):
+            worth, contrast = sums[half]
+            name = "1%d" % half
+            tiles = new_picks(name, HALF)
+            for t in range(PACK):
+                pick(h_second[t], 1, t, HALF * half, tiles)
+            apart1 = make_apart(tiles, name, 2)
+            both1 = make_both(tiles, name, 3)
+            second_stage_pass(worth, contrast, 1, both1, apart1, 0)
+            for pair in range(2):
+                gate = keep.tile([P, 2 * HALF], F32, name="gate%d%d" % (half, pair), tag="gate%d" % pair)
+                nc.scalar.activation(gate[:], contrast[pair][:].rearrange("p u m -> p (u m)"), ACT.Tanh)
+                result = keep.tile([P, 2 * HALF], F32, name="result%d%d" % (half, pair))
+                nc.vector.scalar_tensor_tensor(
+                    result[:], gate[:], 1.0, worth[pair][:].rearrange("p u m -> p (u m)"), ALU.add, ALU.mult
+                )
+                nc.sync.dma_start(
+                    out[2 * P * pair : 2 * P * (pair + 1), HALF * half : HALF * (half + 1)].rearrange(
+                        "(u p) m -> p u m", p=P
+                    ),
+                    result[:].rearrange("p (u m) -> p u m", u=2),
+                )

@@ -33,10 +33,8 @@ def tile_list_balloon_leg_values_kernel(
     with ExitStack() as ctx:
         lists = ctx.enter_context(tc.tile_pool(name="lists", bufs=1))
         keep = ctx.enter_context(tc.tile_pool(name="keep", bufs=1))
-        raws = ctx.enter_context(tc.tile_pool(name="raws", bufs=2))
+        stream = ctx.enter_context(tc.tile_pool(name="stream", bufs=1))
         rounded = ctx.enter_context(tc.tile_pool(name="rounded", bufs=1))
-        rows = ctx.enter_context(tc.tile_pool(name="rows", bufs=8))
-        tables = ctx.enter_context(tc.tile_pool(name="tables", bufs=2))
         picks = ctx.enter_context(tc.tile_pool(name="picks", bufs=1))
         psum = ctx.enter_context(tc.psum_pool(name="psum", bufs=8))
 
@@ -45,65 +43,75 @@ def tile_list_balloon_leg_values_kernel(
         pos2_sb = lists.tile([P, M // 16], U16, name="pos2_sb")
         nc.sync.dma_start(offs_sb[:], offs)
 
-        gain_sb = keep.tile([P, H_PASSES, PACK], F32, name="gain_sb")
-        nc.scalar.dma_start(gain_sb[:], gain.rearrange("(b p t) -> p b t", p=P, t=PACK))
+        def slot_tile(shape, dtype, name, slot):
+            return stream.tile(shape, dtype, name=name, tag="slot%d" % slot, align_bytes=64)
 
-        tab_bytes = keep.tile([P, T], U8, name="tab_bytes")
-        nc.vector.memset(tab_bytes[:].bitcast(I32), 0)
-
-        def load_rows(pool, weight, a, cols, name):
-            raw = pool.tile([P, PACK, BANK], F32, name=name, tag="slot", align_bytes=64)
+        def load_rows(weight, a, cols, name, slot):
+            raw = slot_tile([P, PACK, BANK], F32, name, slot)
             nc.sync.dma_start(raw[:], weight[KP * a : KP * (a + 1), cols].rearrange("(p j) c -> p j c", j=PACK))
             return raw
 
-        def load_table(a):
-            words = tables.tile([P, T], U32, name="tab%d" % a, tag="slot", align_bytes=64)
+        def load_w1(a, b, slot):
+            return load_rows(w1, a, slice(KP * b, KP * (b + 1)), "w1_raw%d%d" % (a, b), slot)
+
+        def load_table(a, slot):
+            words = slot_tile([P, T], U32, "tab%d" % a, slot)
             nc.sync.dma_start(words[:].bitcast(I32), tab_words[a].rearrange("p t i -> p (t i)").bitcast(I32))
             return words
 
-        tab_sb = [load_table(0)]
-        nc.sync.dma_start(pos1_sb[:], pos1)
-        nc.sync.dma_start(pos2_sb[:], pos2)
+        gain_sb = [slot_tile([P, PACK], F32, "gain_sb%d" % b, 1 + 2 * b) for b in range(H_PASSES)]
+        for b in range(H_PASSES):
+            nc.scalar.dma_start(gain_sb[b][:], gain[KP * b : KP * (b + 1)].rearrange("(p t) -> p t", t=PACK))
+        tab_bytes = keep.tile([P, T], U8, name="tab_bytes", tag="v0", align_bytes=64)
+        nc.gpsimd.memset(tab_bytes[:].bitcast(I32), 0)
+        w1_raw = {(0, 0): load_w1(0, 0, 0)}
+        tab_sb = [load_table(0, 2)]
         by_parity = tab_scales.bitcast(I32).rearrange("a (g s) t -> s g a t", s=2)
         for s in range(2):
-            nc.sync.dma_start(tab_bytes[s:P:8, :].bitcast(I32), by_parity[s, :, 0:2, :])
-            nc.sync.dma_start(tab_bytes[4 + s : P : 16, :].bitcast(I32), by_parity[s, :, 2, :])
-        w1_raw = {(0, 0): load_rows(raws, w1, 0, slice(0, KP), "w1_raw00")}
-        for a in range(1, K_PASSES):
-            tab_sb.append(load_table(a))
-            w1_raw[a, 0] = load_rows(raws, w1, a, slice(0, KP), "w1_raw%d0" % a)
-        w3_raw = [load_rows(tables, w3, b, slice(0, N), "w3_raw%d" % b) for b in range(H_PASSES)]
-        for a in range(K_PASSES):
-            w1_raw[a, 1] = load_rows(raws, w1, a, slice(KP, 2 * KP), "w1_raw%d1" % a)
-        w2_codes = raws.tile([P, H_PASSES, 2 * N], U8, name="w2_codes", tag="slot", align_bytes=64)
-        nc.sync.dma_start(w2_codes[:].bitcast(I32), w2_words.bitcast(I32).rearrange("b p c -> p b c"))
-        w2_plane = raws.tile([P, H_PASSES, N], U8, name="w2_plane", tag="slot", align_bytes=64)
-        nc.gpsimd.memset(w2_plane[:].bitcast(I32), 0)
-        for d in range(4):
-            nc.sync.dma_start(
-                w2_plane[32 * d : 32 * d + 4, :, :].bitcast(I32),
-                w2_scales.bitcast(I32)[:, 4 * d : 4 * d + 4, :].rearrange("b q c -> q b c"),
-            )
+            nc.scalar.dma_start(tab_bytes[s:P:8, :].bitcast(I32), by_parity[s, :, 0:2, :])
+            nc.scalar.dma_start(tab_bytes[4 + s : P : 16, :].bitcast(I32), by_parity[s, :, 2, :])
+        nc.sync.dma_start(pos1_sb[:], pos1)
+        nc.sync.dma_start(pos2_sb[:], pos2)
 
-        half_gain = keep.tile([P, H_PASSES * PACK], F32, name="half_gain")
-        nc.vector.tensor_scalar_mul(half_gain[:], gain_sb[:].rearrange("p b t -> p (b t)"), 0.5)
+        half_gain = [keep.tile([P, PACK], F32, name="half_gain%d" % b) for b in range(H_PASSES)]
+        for b in range(H_PASSES):
+            nc.vector.tensor_scalar_mul(half_gain[b][:], gain_sb[b][:], 0.5)
         gain_rows = []
 
         def spread_gain(b, width):
-            for r in range(PACK * b, PACK * (b + 1)):
-                g = keep.tile([P, width], F32, name="gain_row%d" % r)
-                nc.scalar.copy(g[:], half_gain[:, r : r + 1].to_broadcast([P, width]))
+            for t in range(PACK):
+                g = keep.tile([P, width], F32, name="gain_row%d%d" % (b, t))
+                nc.scalar.copy(g[:], half_gain[b][:, t : t + 1].to_broadcast([P, width]))
                 gain_rows.append(g)
 
         spread_gain(0, M)
 
         picked_bytes = keep.tile([P, S], U8, name="picked_bytes")
         nc.vector.tensor_copy(picked_bytes[:], tab_bytes[:].indirect(offs_sb[:]))
+        w1_raw[1, 0] = load_w1(1, 0, 1)
+        tab_sb.append(load_table(1, 3))
         v_plane = keep.tile([P, S], U8, name="v_plane", align_bytes=64)
         nc.vector.tensor_copy(v_plane[:].bitcast(I32), picked_bytes[:].bitcast(I32))
         for s in range(2):
-            nc.sync.dma_start(
+            nc.gpsimd.dma_start(
                 v_plane[2 + s : 110 : 4, :].bitcast(I32), picked_bytes[16 + s : 124 : 4, :].bitcast(I32)
+            )
+
+        w1_raw[2, 0] = load_w1(2, 0, 0)
+        tab_sb.append(load_table(2, 2))
+        w3_raw = [load_rows(w3, 0, slice(0, N), "w3_raw0", 1)]
+        w1_raw[0, 1] = load_w1(0, 1, 3)
+        w1_raw[1, 1] = load_w1(1, 1, 0)
+        w1_raw[2, 1] = load_w1(2, 1, 2)
+        w3_raw.append(load_rows(w3, 1, slice(0, N), "w3_raw1", 1))
+        w2_codes = slot_tile([P, H_PASSES, 2 * N], U8, "w2_codes", 3)
+        nc.sync.dma_start(w2_codes[:].bitcast(I32), w2_words.bitcast(I32).rearrange("b p c -> p b c"))
+        w2_plane = slot_tile([P, H_PASSES, N], U8, "w2_plane", 0)
+        nc.vector.memset(w2_plane[:].bitcast(I32), 0)
+        for d in range(4):
+            nc.sync.dma_start(
+                w2_plane[32 * d : 32 * d + 4, :, :].bitcast(I32),
+                w2_scales.bitcast(I32)[:, 4 * d : 4 * d + 4, :].rearrange("b q c -> q b c"),
             )
 
         def quantize(source, name):
@@ -114,10 +122,10 @@ def tile_list_balloon_leg_values_kernel(
             return codes, plane
 
         def rounded_tile(width, name, slot):
-            return rounded.tile([P, PACK * width], BF16, name=name, tag="bf%d" % slot, align_bytes=64)
+            return rounded.tile([P, PACK * width], BF16, name=name, tag=slot, align_bytes=64)
 
-        def round_w1(a, b, copy):
-            dealt = rounded_tile(BANK, "w1_bf%d%d" % (a, b), (K_PASSES * b + a) % 2)
+        def round_w1(a, b, copy, slot):
+            dealt = rounded_tile(BANK, "w1_bf%d%d" % (a, b), slot)
             copy(
                 dealt[:].rearrange("p (t m j) -> p m j t", t=PACK, j=PACK),
                 w1_raw[a, b][:].rearrange("p j (m t) -> p m j t", t=PACK),
@@ -135,21 +143,22 @@ def tile_list_balloon_leg_values_kernel(
         def apart_rows(tile):
             return tile.rearrange("p t (c i) -> p c t i", i=4)
 
-        def first_stage_pass(banks, a, w1_q):
-            codes, plane = w1_q
+        def first_stage(banks, w1_q):
             for t in range(PACK):
                 cols = slice(P * t, P * (t + 1))
-                for half in range(S // BANK):
-                    j = slice(BANK * half, BANK * (half + 1))
-                    nc.tensor.matmul_mx(
-                        out=banks[t][half][:],
-                        lhsT=codes[:, cols].bitcast(FP8X4),
-                        lhsT_scale=plane[:, cols],
-                        rhs=v_codes[a][:, j].bitcast(FP8X4),
-                        rhs_scale=v_plane[SCALE_ROW[a] : P, j],
-                        start=(a == 0),
-                        stop=(a == K_PASSES - 1),
-                    )
+                for a in range(K_PASSES):
+                    codes, plane = w1_q[a]
+                    for half in range(S // BANK):
+                        j = slice(BANK * half, BANK * (half + 1))
+                        nc.tensor.matmul_mx(
+                            out=banks[t][half][:],
+                            lhsT=codes[:, cols].bitcast(FP8X4),
+                            lhsT_scale=plane[:, cols],
+                            rhs=v_codes[a][:, j].bitcast(FP8X4),
+                            rhs_scale=v_plane[SCALE_ROW[a] : P, j],
+                            start=(a == 0),
+                            stop=(a == K_PASSES - 1),
+                        )
 
         def new_banks(b):
             return [
@@ -158,7 +167,7 @@ def tile_list_balloon_leg_values_kernel(
             ]
 
         def silu_rows(banks, b, t):
-            h = rows.tile([P, S], F32, name="h%d%d" % (b, t), tag="h")
+            h = rounded.tile([P, S], F32, name="h%d%d" % (b, t), tag="h%d%d" % (b, t), align_bytes=64)
             for half in range(S // BANK):
                 nc.scalar.activation(h[:, BANK * half : BANK * (half + 1)], banks[t][half][:], ACT.Silu)
             return h
@@ -170,56 +179,60 @@ def tile_list_balloon_leg_values_kernel(
                 picks.tile([P, PACK, width], F32, name="diff" + name),
             ]
 
-        def pick(h, b, t, m0, tiles):
+        def pick(h, b, t, tiles, m0, m1):
             climb, descent, diff = tiles
-            width = climb.shape[2]
-            g = gain_rows[PACK * b + t][:, 0:width]
+            g = gain_rows[PACK * b + t][:, m0:m1]
             for dst, pos in ((climb, pos1_sb), (descent, pos2_sb)):
-                nc.vector.tensor_tensor(
-                    dst[:, t, :], h[:].indirect(pos[:, m0 // 16 : (m0 + width) // 16]), g, ALU.mult
-                )
-            nc.vector.tensor_tensor(diff[:, t, :], climb[:, t, :], descent[:, t, :], ALU.subtract)
+                nc.vector.tensor_tensor(dst[:, t, m0:m1], h[:].indirect(pos[:, m0 // 16 : m1 // 16]), g, ALU.mult)
+            nc.vector.tensor_tensor(diff[:, t, m0:m1], climb[:, t, m0:m1], descent[:, t, m0:m1], ALU.subtract)
 
-        def make_both(tiles, name, slot):
+        def make_both(tiles, m0, m1, name, slot):
             climb, descent = tiles[0:2]
-            both = rounded_tile(climb.shape[2], "both" + name, slot)
-            nc.vector.tensor_tensor(woven(both[:]), apart_rows(climb[:]), apart_rows(descent[:]), ALU.add)
+            both = rounded_tile(m1 - m0, "both" + name, slot)
+            nc.vector.tensor_tensor(
+                woven(both[:]), apart_rows(climb[:, :, m0:m1]), apart_rows(descent[:, :, m0:m1]), ALU.add
+            )
             return quantize(both[:], "both" + name)
 
-        def make_apart(tiles, name, slot):
-            diff = tiles[2]
-            width = diff.shape[2]
-            apart = rounded_tile(width, "apart" + name, slot)
-            for m0 in range(0, width, HALF):
+        def make_apart(tiles, m0, m1, name, slot):
+            apart = rounded_tile(m1 - m0, "apart" + name, slot)
+            for c in range(m0, m1, HALF):
                 nc.scalar.activation(
-                    woven(apart[:, PACK * m0 : PACK * (m0 + HALF)]), apart_rows(diff[:, :, m0 : m0 + HALF]), ACT.Abs
+                    woven(apart[:, PACK * (c - m0) : PACK * (c - m0 + HALF)]),
+                    apart_rows(tiles[2][:, :, c : c + HALF]),
+                    ACT.Abs,
                 )
             return quantize(apart[:], "apart" + name)
 
         v_codes = []
+        w1_first = []
         first_banks = new_banks(0)
         for a in range(K_PASSES):
-            picked = keep.tile([P, S], U32, name="v%d" % a, align_bytes=64)
-            nc.vector.tensor_copy(picked[:], tab_sb[a][:].indirect(offs_sb[:]))
-            v_codes.append(picked)
             copy = nc.vector.tensor_copy if a == K_PASSES - 1 else nc.scalar.copy
-            first_stage_pass(first_banks, a, round_w1(a, 0, copy))
-        w3_q = [round_w3(0, nc.vector.tensor_copy, 2)]
-        spread_gain(1, HALF)
+            w1_first.append(round_w1(a, 0, copy, "bf%d" % (a % 2)))
+            picked = keep.tile([P, S], U32, name="v%d" % a, tag="v%d" % a, align_bytes=64)
+            for half in range(S // BANK):
+                nc.vector.tensor_copy(
+                    picked[:, BANK * half : BANK * (half + 1)],
+                    tab_sb[a][:].indirect(offs_sb[:, BANK // 16 * half : BANK // 16 * (half + 1)]),
+                )
+            v_codes.append(picked)
+        first_stage(first_banks, w1_first)
+        w3_q = [round_w3(0, nc.vector.tensor_copy, "bf1")]
+        spread_gain(1, M)
 
         first_picks = new_picks("0", M)
         w1_q = []
         for t in range(PACK):
-            pick(silu_rows(first_banks, 0, t), 0, t, 0, first_picks)
+            pick(silu_rows(first_banks, 0, t), 0, t, first_picks, 0, M)
             if t > 0:
-                w1_q.append(round_w1(t - 1, 1, nc.scalar.copy))
+                w1_q.append(round_w1(t - 1, 1, nc.scalar.copy, "h0%d" % (t - 1)))
         second_banks = new_banks(1)
-        for a in range(K_PASSES):
-            first_stage_pass(second_banks, a, w1_q[a])
-        both0 = make_both(first_picks, "0", 1)
+        first_stage(second_banks, w1_q)
+        both0 = make_both(first_picks, 0, M, "0", "h02")
         h_second = [silu_rows(second_banks, 1, t) for t in range(PACK)]
-        apart0 = make_apart(first_picks, "0", 0)
-        w3_q.append(round_w3(1, nc.scalar.copy, 1))
+        apart0 = make_apart(first_picks, 0, M, "0", "h01")
+        w3_q.append(round_w3(1, nc.scalar.copy, "h02"))
 
         def second_stage_pass(worth, contrast, b, both_q, apart_q, m0):
             for pair in range(2):
@@ -252,6 +265,10 @@ def tile_list_balloon_leg_values_kernel(
                         stop=(b == H_PASSES - 1 and u == 1),
                     )
 
+        second_picks = new_picks("1", M)
+        for t in range(PACK - 1):
+            pick(h_second[t], 1, t, second_picks, 0, M)
+
         sums = []
         for half in range(2):
             worth = [psum.tile([P, 2, HALF], F32, name="worth%d%d" % (half, pair), tag="bank") for pair in range(2)]
@@ -264,11 +281,10 @@ def tile_list_balloon_leg_values_kernel(
         for half in range(2):
             worth, contrast = sums[half]
             name = "1%d" % half
-            tiles = new_picks(name, HALF)
-            for t in range(PACK):
-                pick(h_second[t], 1, t, HALF * half, tiles)
-            apart1 = make_apart(tiles, name, 2)
-            both1 = make_both(tiles, name, 3)
+            m0, m1 = HALF * half, HALF * (half + 1)
+            pick(h_second[PACK - 1], 1, PACK - 1, second_picks, m0, m1)
+            apart1 = make_apart(second_picks, m0, m1, name, "apart" + name)
+            both1 = make_both(second_picks, m0, m1, name, "bf%d" % half)
             second_stage_pass(worth, contrast, 1, both1, apart1, 0)
             for pair in range(2):
                 gate = keep.tile([P, 2 * HALF], F32, name="gate%d%d" % (half, pair), tag="gate%d" % pair)

@@ -20,10 +20,20 @@ P = 128
 PACK = 4
 KP = P * PACK
 BANK = 512
+GROUP = 16
+QUAD = 32
 K_PASSES = K // KP
 H_PASSES = H // KP
-SCALE_ROW = (0, 8, 4)
 HALF = M // 2
+PLANE_ROW = (0, 8, 4)
+
+
+def woven(tile):
+    return tile.rearrange("p (c i t) -> p c t i", i=4, t=PACK)
+
+
+def by_rows(tile):
+    return tile.rearrange("p t (c i) -> p c t i", i=4)
 
 
 def tile_list_balloon_leg_values_kernel(
@@ -32,22 +42,14 @@ def tile_list_balloon_leg_values_kernel(
     nc = tc.nc
     with ExitStack() as ctx:
         lists = ctx.enter_context(tc.tile_pool(name="lists", bufs=1))
-        keep = ctx.enter_context(tc.tile_pool(name="keep", bufs=1))
-        stream = ctx.enter_context(tc.tile_pool(name="stream", bufs=1))
-        rounded = ctx.enter_context(tc.tile_pool(name="rounded", bufs=1))
-        picks = ctx.enter_context(tc.tile_pool(name="picks", bufs=1))
-        psum = ctx.enter_context(tc.psum_pool(name="psum", bufs=8))
+        sbuf = ctx.enter_context(tc.tile_pool(name="sbuf", bufs=1))
+        psum = ctx.enter_context(tc.psum_pool(name="psum", bufs=1))
 
-        offs_sb = lists.tile([P, S // 16], U16, name="offs_sb")
-        pos1_sb = lists.tile([P, M // 16], U16, name="pos1_sb")
-        pos2_sb = lists.tile([P, M // 16], U16, name="pos2_sb")
-        nc.sync.dma_start(offs_sb[:], offs)
-
-        def slot_tile(shape, dtype, name, slot):
-            return stream.tile(shape, dtype, name=name, tag="slot%d" % slot, align_bytes=64)
+        def new(shape, dtype, name, slot=None):
+            return sbuf.tile(shape, dtype, name=name, tag=slot or name, align_bytes=64)
 
         def load_rows(weight, a, cols, name, slot):
-            raw = slot_tile([P, PACK, BANK], F32, name, slot)
+            raw = new([P, PACK, BANK], F32, name, slot)
             nc.sync.dma_start(raw[:], weight[KP * a : KP * (a + 1), cols].rearrange("(p j) c -> p j c", j=PACK))
             return raw
 
@@ -55,196 +57,83 @@ def tile_list_balloon_leg_values_kernel(
             return load_rows(w1, a, slice(KP * b, KP * (b + 1)), "w1_raw%d%d" % (a, b), slot)
 
         def load_table(a, slot):
-            words = slot_tile([P, T], U32, "tab%d" % a, slot)
+            words = new([P, T], U32, "tab%d" % a, slot)
             nc.sync.dma_start(words[:].bitcast(I32), tab_words[a].rearrange("p t i -> p (t i)").bitcast(I32))
             return words
 
-        gain_sb = [slot_tile([P, PACK], F32, "gain_sb%d" % b, 1 + 2 * b) for b in range(H_PASSES)]
-        for b in range(H_PASSES):
-            nc.scalar.dma_start(gain_sb[b][:], gain[KP * b : KP * (b + 1)].rearrange("(p t) -> p t", t=PACK))
-        tab_bytes = keep.tile([P, T], U8, name="tab_bytes", tag="v0", align_bytes=64)
-        nc.gpsimd.memset(tab_bytes[:].bitcast(I32), 0)
-        w1_raw = {(0, 0): load_w1(0, 0, 0)}
-        tab_sb = [load_table(0, 2)]
-        by_parity = tab_scales.bitcast(I32).rearrange("a (g s) t -> s g a t", s=2)
-        for s in range(2):
-            nc.scalar.dma_start(tab_bytes[s:P:8, :].bitcast(I32), by_parity[s, :, 0:2, :])
-            nc.scalar.dma_start(tab_bytes[4 + s : P : 16, :].bitcast(I32), by_parity[s, :, 2, :])
-        nc.sync.dma_start(pos1_sb[:], pos1)
-        nc.sync.dma_start(pos2_sb[:], pos2)
-
-        half_gain = [keep.tile([P, PACK], F32, name="half_gain%d" % b) for b in range(H_PASSES)]
-        for b in range(H_PASSES):
-            nc.vector.tensor_scalar_mul(half_gain[b][:], gain_sb[b][:], 0.5)
-        gain_rows = []
-
-        def spread_gain(b, width):
-            for t in range(PACK):
-                g = keep.tile([P, width], F32, name="gain_row%d%d" % (b, t))
-                nc.scalar.copy(g[:], half_gain[b][:, t : t + 1].to_broadcast([P, width]))
-                gain_rows.append(g)
-
-        spread_gain(0, M)
-
-        picked_bytes = keep.tile([P, S], U8, name="picked_bytes")
-        nc.vector.tensor_copy(picked_bytes[:], tab_bytes[:].indirect(offs_sb[:]))
-        w1_raw[1, 0] = load_w1(1, 0, 1)
-        tab_sb.append(load_table(1, 3))
-        v_plane = keep.tile([P, S], U8, name="v_plane", align_bytes=64)
-        nc.vector.tensor_copy(v_plane[:].bitcast(I32), picked_bytes[:].bitcast(I32))
-        for s in range(2):
-            nc.gpsimd.dma_start(
-                v_plane[2 + s : 110 : 4, :].bitcast(I32), picked_bytes[16 + s : 124 : 4, :].bitcast(I32)
-            )
-
-        w1_raw[2, 0] = load_w1(2, 0, 0)
-        tab_sb.append(load_table(2, 2))
-        w3_raw = [load_rows(w3, 0, slice(0, N), "w3_raw0", 1)]
-        w1_raw[0, 1] = load_w1(0, 1, 3)
-        w1_raw[1, 1] = load_w1(1, 1, 0)
-        w1_raw[2, 1] = load_w1(2, 1, 2)
-        w3_raw.append(load_rows(w3, 1, slice(0, N), "w3_raw1", 1))
-        w2_codes = slot_tile([P, H_PASSES, 2 * N], U8, "w2_codes", 3)
-        nc.sync.dma_start(w2_codes[:].bitcast(I32), w2_words.bitcast(I32).rearrange("b p c -> p b c"))
-        w2_plane = slot_tile([P, H_PASSES, N], U8, "w2_plane", 0)
-        nc.vector.memset(w2_plane[:].bitcast(I32), 0)
-        for d in range(4):
-            nc.sync.dma_start(
-                w2_plane[32 * d : 32 * d + 4, :, :].bitcast(I32),
-                w2_scales.bitcast(I32)[:, 4 * d : 4 * d + 4, :].rearrange("b q c -> q b c"),
-            )
-
         def quantize(source, name):
             width = source.shape[1] // PACK
-            codes = keep.tile([P, width], U32, name=name + "_codes", align_bytes=64)
-            plane = keep.tile([P, width], U8, name=name + "_plane", align_bytes=64)
+            codes = new([P, width], U32, name + "_codes")
+            plane = new([P, width], U8, name + "_plane")
             nc.vector.quantize_mx(out=codes[:].bitcast(FP8X4), scales=plane[:], in_=source)
             return codes, plane
 
-        def rounded_tile(width, name, slot):
-            return rounded.tile([P, PACK * width], BF16, name=name, tag=slot, align_bytes=64)
-
-        def round_w1(a, b, copy, slot):
-            dealt = rounded_tile(BANK, "w1_bf%d%d" % (a, b), slot)
-            copy(
-                dealt[:].rearrange("p (t m j) -> p m j t", t=PACK, j=PACK),
-                w1_raw[a, b][:].rearrange("p j (m t) -> p m j t", t=PACK),
-            )
+        def round_w1(a, b, copies, slot):
+            dealt = new([P, PACK * BANK], BF16, "w1_bf%d%d" % (a, b), slot)
+            dst = dealt[:].rearrange("p (t m j) -> p m j t", t=PACK, j=PACK)
+            src = w1_raw[a, b][:].rearrange("p j (m t) -> p m j t", t=PACK)
+            share = P // len(copies)
+            for i, copy in enumerate(copies):
+                copy(dst[:, share * i : share * (i + 1)], src[:, share * i : share * (i + 1)])
             return quantize(dealt[:], "w1_%d%d" % (a, b))
 
         def round_w3(b, copy, slot):
-            w3_bf = rounded_tile(N, "w3_bf%d" % b, slot)
-            copy(woven(w3_bf[:]), apart_rows(w3_raw[b][:]))
+            w3_bf = new([P, PACK * N], BF16, "w3_bf%d" % b, slot)
+            copy(woven(w3_bf[:]), by_rows(w3_raw[b][:]))
             return quantize(w3_bf[:], "w3_%d" % b)
 
-        def woven(tile):
-            return tile.rearrange("p (c i t) -> p c t i", i=4, t=PACK)
-
-        def apart_rows(tile):
-            return tile.rearrange("p t (c i) -> p c t i", i=4)
-
-        def first_stage(banks, w1_q):
+        def first_stage(b, w1_q):
+            slices_in_psum = PACK if b == 0 else PACK // 2
+            banks = [
+                [
+                    psum.tile([P, BANK], F32, name="acc%d%d%d" % (b, t, u), tag="bank%d%d" % (t % slices_in_psum, u))
+                    for u in range(S // BANK)
+                ]
+                for t in range(PACK)
+            ]
             for t in range(PACK):
                 cols = slice(P * t, P * (t + 1))
                 for a in range(K_PASSES):
                     codes, plane = w1_q[a]
-                    for half in range(S // BANK):
-                        j = slice(BANK * half, BANK * (half + 1))
+                    for u in range(S // BANK):
+                        j = slice(BANK * u, BANK * (u + 1))
                         nc.tensor.matmul_mx(
-                            out=banks[t][half][:],
+                            out=banks[t][u][:],
                             lhsT=codes[:, cols].bitcast(FP8X4),
                             lhsT_scale=plane[:, cols],
                             rhs=v_codes[a][:, j].bitcast(FP8X4),
-                            rhs_scale=v_plane[SCALE_ROW[a] : P, j],
+                            rhs_scale=v_plane[PLANE_ROW[a] : P, j],
                             start=(a == 0),
                             stop=(a == K_PASSES - 1),
                         )
-
-        def new_banks(b):
-            return [
-                [psum.tile([P, BANK], F32, name="acc%d%d%d" % (b, t, half), tag="bank") for half in range(S // BANK)]
-                for t in range(PACK)
-            ]
+            return banks
 
         def silu_rows(banks, b, t):
-            h = rounded.tile([P, S], F32, name="h%d%d" % (b, t), tag="h%d%d" % (b, t), align_bytes=64)
-            for half in range(S // BANK):
-                nc.scalar.activation(h[:, BANK * half : BANK * (half + 1)], banks[t][half][:], ACT.Silu)
+            h = new([P, S], F32, "h%d%d" % (b, t))
+            for u in range(S // BANK):
+                nc.scalar.activation(h[:, BANK * u : BANK * (u + 1)], banks[t][u][:], ACT.Silu)
             return h
 
-        def new_picks(name, width):
-            return [
-                picks.tile([P, PACK, width], F32, name="climb" + name, tag="climb"),
-                picks.tile([P, PACK, width], F32, name="descent" + name, tag="descent"),
-                picks.tile([P, PACK, width], F32, name="diff" + name),
-            ]
-
-        def pick(h, b, t, tiles, m0, m1):
-            climb, descent, diff = tiles
-            g = gain_rows[PACK * b + t][:, m0:m1]
-            for dst, pos in ((climb, pos1_sb), (descent, pos2_sb)):
-                nc.vector.tensor_tensor(dst[:, t, m0:m1], h[:].indirect(pos[:, m0 // 16 : m1 // 16]), g, ALU.mult)
-            nc.vector.tensor_tensor(diff[:, t, m0:m1], climb[:, t, m0:m1], descent[:, t, m0:m1], ALU.subtract)
-
-        def make_both(tiles, m0, m1, name, slot):
-            climb, descent = tiles[0:2]
-            both = rounded_tile(m1 - m0, "both" + name, slot)
+        def add_woven(first, second, m0, m1, name, slot=None):
+            both = new([P, PACK * (m1 - m0)], BF16, name, slot)
             nc.vector.tensor_tensor(
-                woven(both[:]), apart_rows(climb[:, :, m0:m1]), apart_rows(descent[:, :, m0:m1]), ALU.add
+                woven(both[:]), by_rows(first[:, :, m0:m1]), by_rows(second[:, :, m0:m1]), ALU.add
             )
-            return quantize(both[:], "both" + name)
+            return quantize(both[:], name)
 
-        def make_apart(tiles, m0, m1, name, slot):
-            apart = rounded_tile(m1 - m0, "apart" + name, slot)
-            for c in range(m0, m1, HALF):
-                nc.scalar.activation(
-                    woven(apart[:, PACK * (c - m0) : PACK * (c - m0 + HALF)]),
-                    apart_rows(tiles[2][:, :, c : c + HALF]),
-                    ACT.Abs,
-                )
-            return quantize(apart[:], "apart" + name)
-
-        v_codes = []
-        w1_first = []
-        first_banks = new_banks(0)
-        for a in range(K_PASSES):
-            copy = nc.vector.tensor_copy if a == K_PASSES - 1 else nc.scalar.copy
-            w1_first.append(round_w1(a, 0, copy, "bf%d" % (a % 2)))
-            picked = keep.tile([P, S], U32, name="v%d" % a, tag="v%d" % a, align_bytes=64)
-            for half in range(S // BANK):
-                nc.vector.tensor_copy(
-                    picked[:, BANK * half : BANK * (half + 1)],
-                    tab_sb[a][:].indirect(offs_sb[:, BANK // 16 * half : BANK // 16 * (half + 1)]),
-                )
-            v_codes.append(picked)
-        first_stage(first_banks, w1_first)
-        w3_q = [round_w3(0, nc.vector.tensor_copy, "bf1")]
-        spread_gain(1, M)
-
-        first_picks = new_picks("0", M)
-        w1_q = []
-        for t in range(PACK):
-            pick(silu_rows(first_banks, 0, t), 0, t, first_picks, 0, M)
-            if t > 0:
-                w1_q.append(round_w1(t - 1, 1, nc.scalar.copy, "h0%d" % (t - 1)))
-        second_banks = new_banks(1)
-        first_stage(second_banks, w1_q)
-        both0 = make_both(first_picks, 0, M, "0", "h02")
-        h_second = [silu_rows(second_banks, 1, t) for t in range(PACK)]
-        apart0 = make_apart(first_picks, 0, M, "0", "h01")
-        w3_q.append(round_w3(1, nc.scalar.copy, "h02"))
+        def abs_woven(apart, diff, m0):
+            nc.scalar.activation(woven(apart), by_rows(diff[:, :, m0 : m0 + HALF]), ACT.Abs)
 
         def second_stage_pass(worth, contrast, b, both_q, apart_q, m0):
             for pair in range(2):
                 for u in range(2):
                     nt = 2 * pair + u
-                    n_cols = slice(P * nt, P * (nt + 1))
                     for c in range(HALF // P):
                         m_cols = slice(m0 + P * c, m0 + P * (c + 1))
                         nc.tensor.matmul_mx(
                             out=worth[pair][:, u, P * c : P * (c + 1)],
                             lhsT=w2_codes[:, b, 2 * P * nt : 2 * P * (nt + 1)].bitcast(FP4X4),
-                            lhsT_scale=w2_plane[:, b, n_cols],
+                            lhsT_scale=w2_plane[:, b, P * nt : P * (nt + 1)],
                             rhs=both_q[0][:, m_cols].bitcast(FP8X4),
                             rhs_scale=both_q[1][:, m_cols],
                             start=(b == 0 and u == 0 and c == 0),
@@ -252,50 +141,170 @@ def tile_list_balloon_leg_values_kernel(
                         )
             for pair in range(2):
                 for u in range(2):
-                    nt = 2 * pair + u
-                    n_cols = slice(P * nt, P * (nt + 1))
-                    m_cols = slice(m0, m0 + HALF)
+                    n_cols = slice(P * (2 * pair + u), P * (2 * pair + u + 1))
                     nc.tensor.matmul_mx(
                         out=contrast[pair][:, u, :],
                         lhsT=w3_q[b][0][:, n_cols].bitcast(FP8X4),
                         lhsT_scale=w3_q[b][1][:, n_cols],
-                        rhs=apart_q[0][:, m_cols].bitcast(FP8X4),
-                        rhs_scale=apart_q[1][:, m_cols],
+                        rhs=apart_q[0][:, m0 : m0 + HALF].bitcast(FP8X4),
+                        rhs_scale=apart_q[1][:, m0 : m0 + HALF],
                         start=(b == 0 and u == 0),
                         stop=(b == H_PASSES - 1 and u == 1),
                     )
 
-        second_picks = new_picks("1", M)
-        for t in range(PACK - 1):
-            pick(h_second[t], 1, t, second_picks, 0, M)
+        offs_sb = lists.tile([P, S // GROUP], U16, name="offs_sb")
+        pos1_sb = lists.tile([P, M // GROUP], U16, name="pos1_sb")
+        pos2_sb = lists.tile([P, M // GROUP], U16, name="pos2_sb")
+        nc.sync.dma_start(offs_sb[:], offs)
+        nc.sync.dma_start(pos1_sb[:], pos1)
+        nc.sync.dma_start(pos2_sb[:], pos2)
+
+        gain_sb = [new([P, PACK], F32, "gain_sb%d" % b, "load%d" % (1 + b)) for b in range(H_PASSES)]
+        for b in range(H_PASSES):
+            nc.scalar.dma_start(gain_sb[b][:], gain[KP * b : KP * (b + 1)].rearrange("(p t) -> p t", t=PACK))
+
+        tab_bytes = new([P, T], U8, "tab_bytes", "v0")
+        nc.gpsimd.memset(tab_bytes[:].bitcast(I32), 0)
+        w1_raw = {(0, 0): load_w1(0, 0, "load0")}
+        by_parity = tab_scales.bitcast(I32).rearrange("a (g s) t -> s g a t", s=2)
+        for s in range(2):
+            nc.sync.dma_start(tab_bytes[s : P : PLANE_ROW[1], :].bitcast(I32), by_parity[s, :, 0:2, :])
+            nc.sync.dma_start(tab_bytes[PLANE_ROW[2] + s : P : GROUP, :].bitcast(I32), by_parity[s, :, 2, :])
+
+        half_gain = [new([P, 1], F32, "half_gain%d" % r, "load3" if r == 0 else None) for r in range(H // P)]
+        for r in range(H // P):
+            nc.vector.tensor_scalar_mul(half_gain[r][:], gain_sb[r // PACK][:, r % PACK : r % PACK + 1], 0.5)
+        gain_rows = [new([P, M], F32, "gain_row%d" % t) for t in range(PACK)]
+        for t in range(PACK):
+            nc.scalar.copy(gain_rows[t][:], half_gain[t][:].to_broadcast([P, M]))
+
+        picked_bytes = new([P, S], U8, "picked_bytes")
+        nc.vector.tensor_copy(picked_bytes[:], tab_bytes[:].indirect(offs_sb[:]))
+        tab_sb = [load_table(0, "load1")]
+        w1_raw[1, 0] = load_w1(1, 0, "load2")
+        tab_sb.append(load_table(1, "load3"))
+        v_plane = new([P, S], U8, "v_plane")
+        nc.vector.tensor_copy(v_plane[:].bitcast(I32), picked_bytes[:].bitcast(I32))
+        for row in PLANE_ROW:
+            for s in range(2):
+                nc.sync.dma_start(
+                    v_plane[row + 2 + s : P : QUAD, :].bitcast(I32),
+                    picked_bytes[GROUP + row + s : P : QUAD, :].bitcast(I32),
+                )
+
+        w1_q = [round_w1(0, 0, [nc.scalar.copy], "bf0")]
+        w1_raw[2, 0] = load_w1(2, 0, "load0")
+        tab_sb.append(load_table(2, "load1"))
+        w3_raw = [load_rows(w3, 0, slice(0, N), "w3_raw0", "load2")]
+        w1_raw[0, 1] = load_w1(0, 1, "load3")
+        w1_raw[1, 1] = load_w1(1, 1, "load0")
+        w1_raw[2, 1] = load_w1(2, 1, "load1")
+        w3_raw.append(load_rows(w3, 1, slice(0, N), "w3_raw1", "load2"))
+        w2_plane = new([P, H_PASSES, N], U8, "w2_plane", "load0")
+        nc.gpsimd.memset(w2_plane[:].bitcast(I32), 0)
+        for d in range(P // QUAD):
+            nc.sync.dma_start(
+                w2_plane[QUAD * d : QUAD * d + 4, :, :].bitcast(I32),
+                w2_scales.bitcast(I32)[:, 4 * d : 4 * d + 4, :].rearrange("b q c -> q b c"),
+            )
+        w2_codes = new([P, H_PASSES, 2 * N], U8, "w2_codes", "load3")
+        nc.sync.dma_start(w2_codes[:].bitcast(I32), w2_words.bitcast(I32).rearrange("b p c -> p b c"))
+
+        v_codes = []
+        for a in range(K_PASSES):
+            if a > 0:
+                copies = [nc.scalar.copy, nc.vector.tensor_copy] if a == K_PASSES - 1 else [nc.scalar.copy]
+                w1_q.append(round_w1(a, 0, copies, "bf%d" % (a % 2)))
+            picked = new([P, S], U32, "v%d" % a)
+            for u in range(S // BANK):
+                nc.vector.tensor_copy(
+                    picked[:, BANK * u : BANK * (u + 1)],
+                    tab_sb[a][:].indirect(offs_sb[:, BANK // GROUP * u : BANK // GROUP * (u + 1)]),
+                )
+            v_codes.append(picked)
+        banks = first_stage(0, w1_q)
+        w3_q = [round_w3(0, nc.vector.tensor_copy, "bf1")]
+
+        legs = new([P, 2, PACK, M], F32, "legs0", "bf1")
+        w1_q = []
+        for t in range(PACK):
+            h = silu_rows(banks, 0, t)
+            for leg, pos in enumerate((pos1_sb, pos2_sb)):
+                nc.vector.tensor_tensor(legs[:, leg, t, :], h[:].indirect(pos[:]), gain_rows[t][:], ALU.mult)
+            if t > 0:
+                w1_q.append(round_w1(t - 1, 1, [nc.scalar.copy], ("bf0", "h00", "h01")[t - 1]))
+        banks = first_stage(1, w1_q)
+        diff = new([P, PACK, M], F32, "diff0", "load1")
+        nc.vector.tensor_tensor(diff[:], legs[:, 0], legs[:, 1], ALU.subtract)
+        both0 = add_woven(legs[:, 0], legs[:, 1], 0, M, "both0", "h01")
+
+        apart = new([P, PACK * M], BF16, "apart0")
+        h_second = []
+        for t in range(PACK):
+            h = silu_rows(banks, 1, t)
+            for u in range(S // BANK):
+                j = slice(BANK * u, BANK * (u + 1))
+                nc.scalar.activation(h[:, j], h[:, j], ACT.Copy, scale=half_gain[PACK + t][:])
+            h_second.append(h)
+            if t in (1, 2):
+                m0 = HALF * (t - 1)
+                abs_woven(apart[:, PACK * m0 : PACK * (m0 + HALF)], diff, m0)
+        apart0 = quantize(apart[:], "apart0")
+        w3_q.append(round_w3(1, nc.scalar.copy, "bf0"))
+
+        legs = new([P, 2, PACK, M], F32, "legs1", "bf1")
+        climb, twice = legs[:, 0], legs[:, 1]
+        diff = new([P, PACK, M], F32, "diff1")
+
+        def pick_pairs(t, m0, m1):
+            cols = slice(m0 // GROUP, m1 // GROUP)
+            window = h_second[t][:]
+            nc.vector.tensor_copy(climb[:, t, m0:m1], window.indirect(pos1_sb[:, cols]))
+            nc.vector.tensor_tensor(
+                diff[:, t, m0:m1], window.indirect(pos2_sb[:, cols]), climb[:, t, m0:m1], ALU.subtract
+            )
+
+        last = PACK - 1
+        for t in range(last):
+            pick_pairs(t, 0, M)
+            nc.scalar.activation(twice[:, t, :], climb[:, t, :], ACT.Copy, scale=2.0)
 
         sums = []
         for half in range(2):
-            worth = [psum.tile([P, 2, HALF], F32, name="worth%d%d" % (half, pair), tag="bank") for pair in range(2)]
-            contrast = [
-                psum.tile([P, 2, HALF], F32, name="contrast%d%d" % (half, pair), tag="bank") for pair in range(2)
+            worth, contrast = [
+                [
+                    psum.tile([P, 2, HALF], F32, name="%s%d%d" % (kind, half, pair), tag="bank%d%d" % (row, pair))
+                    for pair in range(2)
+                ]
+                for kind, row in (("worth", 2 - 2 * half), ("contrast", 3 - 2 * half))
             ]
             second_stage_pass(worth, contrast, 0, both0, apart0, HALF * half)
             sums.append((worth, contrast))
 
         for half in range(2):
-            worth, contrast = sums[half]
-            name = "1%d" % half
             m0, m1 = HALF * half, HALF * (half + 1)
-            pick(h_second[PACK - 1], 1, PACK - 1, second_picks, m0, m1)
-            apart1 = make_apart(second_picks, m0, m1, name, "apart" + name)
-            both1 = make_both(second_picks, m0, m1, name, "bf%d" % half)
-            second_stage_pass(worth, contrast, 1, both1, apart1, 0)
+            pick_pairs(last, m0, m1)
+            nc.vector.tensor_scalar_mul(twice[:, last, m0:m1], climb[:, last, m0:m1], 2.0)
+            apart = new([P, PACK * HALF], BF16, "apart1%d" % half)
+            abs_woven(apart[:], diff, m0)
+            apart1 = quantize(apart[:], "apart1%d" % half)
+            both1 = add_woven(twice, diff, m0, m1, "both1%d" % half)
+            second_stage_pass(*sums[half], 1, both1, apart1, 0)
+
+        for half in range(2):
+            worth, contrast = sums[half]
             for pair in range(2):
-                gate = keep.tile([P, 2 * HALF], F32, name="gate%d%d" % (half, pair), tag="gate%d" % pair)
-                nc.scalar.activation(gate[:], contrast[pair][:].rearrange("p u m -> p (u m)"), ACT.Tanh)
-                result = keep.tile([P, 2 * HALF], F32, name="result%d%d" % (half, pair))
-                nc.vector.scalar_tensor_tensor(
-                    result[:], gate[:], 1.0, worth[pair][:].rearrange("p u m -> p (u m)"), ALU.add, ALU.mult
-                )
-                nc.sync.dma_start(
-                    out[2 * P * pair : 2 * P * (pair + 1), HALF * half : HALF * (half + 1)].rearrange(
-                        "(u p) m -> p u m", p=P
-                    ),
-                    result[:].rearrange("p (u m) -> p u m", u=2),
-                )
+                gate = new([P, 2, HALF], F32, "gate%d%d" % (half, pair), "gate%d" % pair)
+                result = new([P, 2, HALF], F32, "result%d%d" % (half, pair))
+                step = 1 if (half, pair) == (1, 1) else 2
+                for u in range(0, 2, step):
+                    part = slice(u, u + step)
+                    nc.scalar.activation(gate[:, part, :], contrast[pair][:, part, :], ACT.Tanh)
+                    nc.vector.scalar_tensor_tensor(
+                        result[:, part, :], gate[:, part, :], 1.0, worth[pair][:, part, :], ALU.add, ALU.mult
+                    )
+                    n0 = P * (2 * pair + u)
+                    nc.sync.dma_start(
+                        out[n0 : n0 + P * step, HALF * half : HALF * (half + 1)].rearrange("(u p) m -> p u m", p=P),
+                        result[:, part, :],
+                    )

from contextlib import ExitStack

import concourse.mybir as mybir

K, H, N, T, S, M = 1536, 1024, 512, 2048, 1024, 512
FLOPS = 2 * K * H * S + 2 * 2 * H * N * M

F32 = mybir.dt.float32
BF16 = mybir.dt.bfloat16
I32 = mybir.dt.int32
U32 = mybir.dt.uint32
U16 = mybir.dt.uint16
U8 = mybir.dt.uint8
FP8X4 = mybir.dt.float8_e4m3fn_x4
FP4X4 = mybir.dt.float4_e2m1fn_x4
ALU = mybir.AluOpType
ACT = mybir.ActivationFunctionType

P = 128
PACK = 4
KP = P * PACK
BANK = 512
GROUP = 16
QUAD = 32
K_PASSES = K // KP
H_PASSES = H // KP
HALF = M // 2
PLANE_ROW = (0, 8, 4)


def woven(tile):
    return tile.rearrange("p (c i t) -> p c t i", i=4, t=PACK)


def by_rows(tile):
    return tile.rearrange("p t (c i) -> p c t i", i=4)


def tile_list_balloon_leg_values_kernel(
    tc, tab_words, tab_scales, offs, pos1, pos2, w1, gain, w2_words, w2_scales, w3, out
):
    nc = tc.nc
    with ExitStack() as ctx:
        lists = ctx.enter_context(tc.tile_pool(name="lists", bufs=1))
        sbuf = ctx.enter_context(tc.tile_pool(name="sbuf", bufs=1))
        psum = ctx.enter_context(tc.psum_pool(name="psum", bufs=1))

        def new(shape, dtype, name, slot=None):
            return sbuf.tile(shape, dtype, name=name, tag=slot or name, align_bytes=64)

        def load_rows(weight, a, cols, name, slot):
            raw = new([P, PACK, BANK], F32, name, slot)
            nc.sync.dma_start(raw[:], weight[KP * a : KP * (a + 1), cols].rearrange("(p j) c -> p j c", j=PACK))
            return raw

        def load_w1(a, b, slot):
            return load_rows(w1, a, slice(KP * b, KP * (b + 1)), "w1_raw%d%d" % (a, b), slot)

        def load_table(a, slot):
            words = new([P, T], U32, "tab%d" % a, slot)
            nc.sync.dma_start(words[:].bitcast(I32), tab_words[a].rearrange("p t i -> p (t i)").bitcast(I32))
            return words

        def quantize(source, name):
            width = source.shape[1] // PACK
            codes = new([P, width], U32, name + "_codes")
            plane = new([P, width], U8, name + "_plane")
            nc.vector.quantize_mx(out=codes[:].bitcast(FP8X4), scales=plane[:], in_=source)
            return codes, plane

        def round_w1(a, b, copies, slot):
            dealt = new([P, PACK * BANK], BF16, "w1_bf%d%d" % (a, b), slot)
            dst = dealt[:].rearrange("p (t m j) -> p m j t", t=PACK, j=PACK)
            src = w1_raw[a, b][:].rearrange("p j (m t) -> p m j t", t=PACK)
            share = P // len(copies)
            for i, copy in enumerate(copies):
                copy(dst[:, share * i : share * (i + 1)], src[:, share * i : share * (i + 1)])
            return quantize(dealt[:], "w1_%d%d" % (a, b))

        def round_w3(b, copy, slot):
            w3_bf = new([P, PACK * N], BF16, "w3_bf%d" % b, slot)
            copy(woven(w3_bf[:]), by_rows(w3_raw[b][:]))
            return quantize(w3_bf[:], "w3_%d" % b)

        def first_stage(b, w1_q):
            slices_in_psum = PACK if b == 0 else PACK // 2
            banks = [
                [
                    psum.tile([P, BANK], F32, name="acc%d%d%d" % (b, t, u), tag="bank%d%d" % (t % slices_in_psum, u))
                    for u in range(S // BANK)
                ]
                for t in range(PACK)
            ]
            for t in range(PACK):
                cols = slice(P * t, P * (t + 1))
                for a in range(K_PASSES):
                    codes, plane = w1_q[a]
                    for u in range(S // BANK):
                        j = slice(BANK * u, BANK * (u + 1))
                        nc.tensor.matmul_mx(
                            out=banks[t][u][:],
                            lhsT=codes[:, cols].bitcast(FP8X4),
                            lhsT_scale=plane[:, cols],
                            rhs=v_codes[a][:, j].bitcast(FP8X4),
                            rhs_scale=v_plane[PLANE_ROW[a] : P, j],
                            start=(a == 0),
                            stop=(a == K_PASSES - 1),
                        )
            return banks

        def silu_rows(banks, b, t):
            h = new([P, S], F32, "h%d%d" % (b, t))
            for u in range(S // BANK):
                nc.scalar.activation(h[:, BANK * u : BANK * (u + 1)], banks[t][u][:], ACT.Silu)
            return h

        def add_woven(first, second, m0, m1, name, slot=None):
            both = new([P, PACK * (m1 - m0)], BF16, name, slot)
            nc.vector.tensor_tensor(
                woven(both[:]), by_rows(first[:, :, m0:m1]), by_rows(second[:, :, m0:m1]), ALU.add
            )
            return quantize(both[:], name)

        def abs_woven(apart, diff, m0):
            nc.scalar.activation(woven(apart), by_rows(diff[:, :, m0 : m0 + HALF]), ACT.Abs)

        def second_stage_pass(worth, contrast, b, both_q, apart_q, m0):
            for pair in range(2):
                for u in range(2):
                    nt = 2 * pair + u
                    for c in range(HALF // P):
                        m_cols = slice(m0 + P * c, m0 + P * (c + 1))
                        nc.tensor.matmul_mx(
                            out=worth[pair][:, u, P * c : P * (c + 1)],
                            lhsT=w2_codes[:, b, 2 * P * nt : 2 * P * (nt + 1)].bitcast(FP4X4),
                            lhsT_scale=w2_plane[:, b, P * nt : P * (nt + 1)],
                            rhs=both_q[0][:, m_cols].bitcast(FP8X4),
                            rhs_scale=both_q[1][:, m_cols],
                            start=(b == 0 and u == 0 and c == 0),
                            stop=(b == H_PASSES - 1 and u == 1 and c == HALF // P - 1),
                        )
            for pair in range(2):
                for u in range(2):
                    n_cols = slice(P * (2 * pair + u), P * (2 * pair + u + 1))
                    nc.tensor.matmul_mx(
                        out=contrast[pair][:, u, :],
                        lhsT=w3_q[b][0][:, n_cols].bitcast(FP8X4),
                        lhsT_scale=w3_q[b][1][:, n_cols],
                        rhs=apart_q[0][:, m0 : m0 + HALF].bitcast(FP8X4),
                        rhs_scale=apart_q[1][:, m0 : m0 + HALF],
                        start=(b == 0 and u == 0),
                        stop=(b == H_PASSES - 1 and u == 1),
                    )

        offs_sb = lists.tile([P, S // GROUP], U16, name="offs_sb")
        pos1_sb = lists.tile([P, M // GROUP], U16, name="pos1_sb")
        pos2_sb = lists.tile([P, M // GROUP], U16, name="pos2_sb")
        nc.sync.dma_start(offs_sb[:], offs)
        nc.sync.dma_start(pos1_sb[:], pos1)
        nc.sync.dma_start(pos2_sb[:], pos2)

        gain_sb = [new([P, PACK], F32, "gain_sb%d" % b, "load%d" % (1 + b)) for b in range(H_PASSES)]
        for b in range(H_PASSES):
            nc.scalar.dma_start(gain_sb[b][:], gain[KP * b : KP * (b + 1)].rearrange("(p t) -> p t", t=PACK))

        tab_bytes = new([P, T], U8, "tab_bytes", "v0")
        nc.gpsimd.memset(tab_bytes[:].bitcast(I32), 0)
        w1_raw = {(0, 0): load_w1(0, 0, "load0")}
        by_parity = tab_scales.bitcast(I32).rearrange("a (g s) t -> s g a t", s=2)
        for s in range(2):
            nc.sync.dma_start(tab_bytes[s : P : PLANE_ROW[1], :].bitcast(I32), by_parity[s, :, 0:2, :])
            nc.sync.dma_start(tab_bytes[PLANE_ROW[2] + s : P : GROUP, :].bitcast(I32), by_parity[s, :, 2, :])

        half_gain = [new([P, 1], F32, "half_gain%d" % r, "load3" if r == 0 else None) for r in range(H // P)]
        for r in range(H // P):
            nc.vector.tensor_scalar_mul(half_gain[r][:], gain_sb[r // PACK][:, r % PACK : r % PACK + 1], 0.5)
        gain_rows = [new([P, M], F32, "gain_row%d" % t) for t in range(PACK)]
        for t in range(PACK):
            nc.scalar.copy(gain_rows[t][:], half_gain[t][:].to_broadcast([P, M]))

        picked_bytes = new([P, S], U8, "picked_bytes")
        nc.vector.tensor_copy(picked_bytes[:], tab_bytes[:].indirect(offs_sb[:]))
        tab_sb = [load_table(0, "load1")]
        w1_raw[1, 0] = load_w1(1, 0, "load2")
        tab_sb.append(load_table(1, "load3"))
        v_plane = new([P, S], U8, "v_plane")
        nc.vector.tensor_copy(v_plane[:].bitcast(I32), picked_bytes[:].bitcast(I32))
        for row in PLANE_ROW:
            for s in range(2):
                nc.sync.dma_start(
                    v_plane[row + 2 + s : P : QUAD, :].bitcast(I32),
                    picked_bytes[GROUP + row + s : P : QUAD, :].bitcast(I32),
                )

        w1_q = [round_w1(0, 0, [nc.scalar.copy], "bf0")]
        w1_raw[2, 0] = load_w1(2, 0, "load0")
        tab_sb.append(load_table(2, "load1"))
        w3_raw = [load_rows(w3, 0, slice(0, N), "w3_raw0", "load2")]
        w1_raw[0, 1] = load_w1(0, 1, "load3")
        w1_raw[1, 1] = load_w1(1, 1, "load0")
        w1_raw[2, 1] = load_w1(2, 1, "load1")
        w3_raw.append(load_rows(w3, 1, slice(0, N), "w3_raw1", "load2"))
        w2_plane = new([P, H_PASSES, N], U8, "w2_plane", "load0")
        nc.gpsimd.memset(w2_plane[:].bitcast(I32), 0)
        for d in range(P // QUAD):
            nc.sync.dma_start(
                w2_plane[QUAD * d : QUAD * d + 4, :, :].bitcast(I32),
                w2_scales.bitcast(I32)[:, 4 * d : 4 * d + 4, :].rearrange("b q c -> q b c"),
            )
        w2_codes = new([P, H_PASSES, 2 * N], U8, "w2_codes", "load3")
        nc.sync.dma_start(w2_codes[:].bitcast(I32), w2_words.bitcast(I32).rearrange("b p c -> p b c"))

        v_codes = []
        for a in range(K_PASSES):
            if a > 0:
                copies = [nc.scalar.copy, nc.vector.tensor_copy] if a == K_PASSES - 1 else [nc.scalar.copy]
                w1_q.append(round_w1(a, 0, copies, "bf%d" % (a % 2)))
            picked = new([P, S], U32, "v%d" % a)
            for u in range(S // BANK):
                nc.vector.tensor_copy(
                    picked[:, BANK * u : BANK * (u + 1)],
                    tab_sb[a][:].indirect(offs_sb[:, BANK // GROUP * u : BANK // GROUP * (u + 1)]),
                )
            v_codes.append(picked)
        banks = first_stage(0, w1_q)
        w3_q = [round_w3(0, nc.vector.tensor_copy, "bf1")]

        legs = new([P, 2, PACK, M], F32, "legs0", "bf1")
        w1_q = []
        for t in range(PACK):
            h = silu_rows(banks, 0, t)
            for leg, pos in enumerate((pos1_sb, pos2_sb)):
                nc.vector.tensor_tensor(legs[:, leg, t, :], h[:].indirect(pos[:]), gain_rows[t][:], ALU.mult)
            if t > 0:
                w1_q.append(round_w1(t - 1, 1, [nc.scalar.copy], ("bf0", "h00", "h01")[t - 1]))
        banks = first_stage(1, w1_q)
        diff = new([P, PACK, M], F32, "diff0", "load1")
        nc.vector.tensor_tensor(diff[:], legs[:, 0], legs[:, 1], ALU.subtract)
        both0 = add_woven(legs[:, 0], legs[:, 1], 0, M, "both0", "h01")

        apart = new([P, PACK * M], BF16, "apart0")
        h_second = []
        for t in range(PACK):
            h = silu_rows(banks, 1, t)
            for u in range(S // BANK):
                j = slice(BANK * u, BANK * (u + 1))
                nc.scalar.activation(h[:, j], h[:, j], ACT.Copy, scale=half_gain[PACK + t][:])
            h_second.append(h)
            if t in (1, 2):
                m0 = HALF * (t - 1)
                abs_woven(apart[:, PACK * m0 : PACK * (m0 + HALF)], diff, m0)
        apart0 = quantize(apart[:], "apart0")
        w3_q.append(round_w3(1, nc.scalar.copy, "bf0"))

        legs = new([P, 2, PACK, M], F32, "legs1", "bf1")
        climb, twice = legs[:, 0], legs[:, 1]
        diff = new([P, PACK, M], F32, "diff1")

        def pick_pairs(t, m0, m1):
            cols = slice(m0 // GROUP, m1 // GROUP)
            window = h_second[t][:]
            nc.vector.tensor_copy(climb[:, t, m0:m1], window.indirect(pos1_sb[:, cols]))
            nc.vector.tensor_tensor(
                diff[:, t, m0:m1], window.indirect(pos2_sb[:, cols]), climb[:, t, m0:m1], ALU.subtract
            )

        last = PACK - 1
        for t in range(last):
            pick_pairs(t, 0, M)
            nc.scalar.activation(twice[:, t, :], climb[:, t, :], ACT.Copy, scale=2.0)

        sums = []
        for half in range(2):
            worth, contrast = [
                [
                    psum.tile([P, 2, HALF], F32, name="%s%d%d" % (kind, half, pair), tag="bank%d%d" % (row, pair))
                    for pair in range(2)
                ]
                for kind, row in (("worth", 2 - 2 * half), ("contrast", 3 - 2 * half))
            ]
            second_stage_pass(worth, contrast, 0, both0, apart0, HALF * half)
            sums.append((worth, contrast))

        for half in range(2):
            m0, m1 = HALF * half, HALF * (half + 1)
            pick_pairs(last, m0, m1)
            nc.vector.tensor_scalar_mul(twice[:, last, m0:m1], climb[:, last, m0:m1], 2.0)
            apart = new([P, PACK * HALF], BF16, "apart1%d" % half)
            abs_woven(apart[:], diff, m0)
            apart1 = quantize(apart[:], "apart1%d" % half)
            both1 = add_woven(twice, diff, m0, m1, "both1%d" % half)
            second_stage_pass(*sums[half], 1, both1, apart1, 0)

        for half in range(2):
            worth, contrast = sums[half]
            for pair in range(2):
                gate = new([P, 2, HALF], F32, "gate%d%d" % (half, pair), "gate%d" % pair)
                result = new([P, 2, HALF], F32, "result%d%d" % (half, pair))
                step = 1 if (half, pair) == (1, 1) else 2
                for u in range(0, 2, step):
                    part = slice(u, u + step)
                    nc.scalar.activation(gate[:, part, :], contrast[pair][:, part, :], ACT.Tanh)
                    nc.vector.scalar_tensor_tensor(
                        result[:, part, :], gate[:, part, :], 1.0, worth[pair][:, part, :], ALU.add, ALU.mult
                    )
                    n0 = P * (2 * pair + u)
                    nc.sync.dma_start(
                        out[n0 : n0 + P * step, HALF * half : HALF * (half + 1)].rearrange("(u p) m -> p u m", p=P),
                        result[:, part, :],
                    )
